import numpy as np
import ml_dtypes


def mxq(x, axis, fmt="e4m3"):
    dtype, down = {"e4m3": (ml_dtypes.float8_e4m3fn, 7), "e5m2": (ml_dtypes.float8_e5m2, 14)}[fmt]
    v = np.moveaxis(np.asarray(x, np.float32).astype(ml_dtypes.bfloat16).astype(np.float64), axis, -1)
    blocks = v.reshape(v.shape[:-1] + (-1, 32))
    amax = np.abs(blocks).max(-1, keepdims=True)
    byte = np.maximum(np.where(amax > 0, np.frexp(amax)[1] - 1 + 127, 0) - down, 1)
    scale = np.exp2(byte - 127.0)
    codes = (blocks / scale).astype(np.float32).astype(dtype).astype(np.float64)
    return np.moveaxis((codes * scale).reshape(v.shape), -1, axis)


WIDE = False


def mx_kscale(k):
    if not WIDE:
        return np.ones(k)
    levels = np.array([10, -10, 5, -5, 0])
    if k % 512:
        return np.exp2(np.random.permutation(np.resize(levels, k // 32))).repeat(32)
    a = np.empty((k // 512, 16))
    for p in range(k // 512):
        a[p, :8] = np.random.permutation(np.resize(levels, 8))
        for g in range(8):
            far = levels[np.abs(levels - a[p, g]) >= 10]
            a[p, g + 8] = far[np.random.randint(len(far))]
    return np.exp2(a.ravel()).repeat(32)


def f64(x):
    return np.asarray(x).astype(np.float64)


def striped(idx):
    return np.tile(idx.reshape(-1, 16).T, (8, 1)).astype(np.uint16)


def unstriped(offs):
    return offs[:16].T.reshape(-1).astype(np.int64)


def pack_weight(w):
    k, n = w.shape
    w = f64(np.asarray(w, np.float32).astype(ml_dtypes.bfloat16)).reshape(k // 32, 32, n)
    amax = np.abs(w).max(1)
    byte = np.clip(np.where(amax > 0, np.frexp(amax)[1] - 1 + 127 - 7, 1), 1, 254)
    scaled = (w * np.exp2(127.0 - byte)[:, None, :]).reshape(k, n).astype(np.float32)
    words = np.ascontiguousarray(scaled.reshape(k // 512, 128, 4, n).transpose(0, 1, 3, 2)).astype(ml_dtypes.float8_e4m3fn).view(np.uint8)
    return words, np.ascontiguousarray(byte.astype(np.uint8).reshape(k // 512, 16, n))


def unpack_weight(words, scales):
    g, p, n, _ = words.shape
    vals = np.ascontiguousarray(words).view(ml_dtypes.float8_e4m3fn).astype(np.float64) * np.repeat(np.exp2(scales.astype(np.float64) - 127.0), 8, axis=1)[..., None]
    return vals.transpose(0, 1, 3, 2).reshape(g * 512, n)


def relu2(v):
    return np.maximum(v, 0.0) ** 2


K, T, E, C, N = 1536, 1024, 4, 128, 384


def by_expert(wq, xq):
    return np.concatenate([wq[e].T @ xq[:, e * C:(e + 1) * C] for e in range(E)], axis=1)


def setup_inputs():
    n = np.random.standard_normal
    s = mx_kscale(K)[:, None]
    packed = [pack_weight(m) for m in n((E, K, N)) / np.sqrt(K) / s[None]]
    return {
        "xT": (n((K, T)) * s).astype(np.float32),
        "w_words": np.stack([m[0] for m in packed]),
        "w_scales": np.stack([m[1] for m in packed]),
        "b": (0.3 * n((N, E))).astype(np.float32),
        "gate": np.tile(np.random.uniform(0.2, 1.0, E * C), (K, 1)).astype(np.float32),
        "offs": striped(np.random.permutation(T)[:E * C]),
    }


def reference(xT, w_words, w_scales, b, gate, offs):
    idx = unstriped(offs)
    w = np.stack([unpack_weight(w_words[e], w_scales[e]) for e in range(E)])
    xq = mxq(f64(gate) * f64(xT)[:, idx], 0, "e4m3")
    y = by_expert(w, xq)
    y = relu2(y + np.repeat(f64(b), C, axis=1))
    out = np.zeros((N, T))
    out[:, idx] = y
    return out

@@ -1,0 +1,165 @@
+from contextlib import ExitStack
+
+import concourse.mybir as mybir
+from concourse.masks import make_identity
+
+K, T, E, C, N = 1536, 1024, 4, 128, 384
+S = E * C
+P = 128
+PACK = 4
+PASSES = K // (P * PACK)
+ROW_BLOCKS = N // P
+
+F32 = mybir.dt.float32
+BF16 = mybir.dt.bfloat16
+I32 = mybir.dt.int32
+U32 = mybir.dt.uint32
+U16 = mybir.dt.uint16
+U8 = mybir.dt.uint8
+FP8X4 = mybir.dt.float8_e4m3fn_x4
+COPY = mybir.ActivationFunctionType.Copy
+RELU = mybir.ActivationFunctionType.Relu
+MULT = mybir.AluOpType.mult
+
+FLOPS = 2 * K * N * S
+BYTES = 4 * K * T + E * K * N + E * K * N // 32 + 4 * N * E + 4 * S + 2 * P * S // 16 + 4 * N * T
+
+UNITS = [(0, 1), (1, 2), (2, 4)]
+
+
+def tile_moe_pre_lin_relu2_kernel(tc, xT, w_words, w_scales, b, gate, offs, out):
+    nc = tc.nc
+    with ExitStack() as ctx:
+        keep = ctx.enter_context(tc.tile_pool(name="keep", bufs=1))
+        psum = ctx.enter_context(tc.psum_pool(name="psum", bufs=1))
+
+        offsets = keep.tile([P, S // 16], U16, name="offsets")
+        ident = keep.tile([P, P], F32, name="ident")
+        gate_rows = keep.tile([P, P], F32, name="gate_rows")
+        gate_cols = keep.tile([P, E], F32, name="gate_cols")
+        bias = keep.tile([P, ROW_BLOCKS, E], F32, name="bias")
+        w_plane = keep.tile([P, E * PASSES * N], U8, name="w_plane", align_bytes=64)
+        w_codes = [keep.tile([P, PASSES, N * PACK], U8, name="w_codes%d" % e, align_bytes=64) for e in range(E)]
+        planes = [[keep.tile([P, T], F32, name="x%d_%d" % (a, t)) for t in range(PACK)] for a in range(PASSES)]
+        picked = [[keep.tile([P, S], F32, name="g%d_%d" % (a, t)) for t in range(PACK)] for a in range(PASSES)]
+        windows = [keep.tile([P, T], F32, name="win%d" % m) for m in range(ROW_BLOCKS)]
+        x_codes = [keep.tile([P, S], U32, name="xc%d" % a, align_bytes=64) for a in range(PASSES)]
+        x_plane = [keep.tile([P, S], U8, name="xs%d" % a, align_bytes=64) for a in range(PASSES)]
+
+        def load_plane(a, t):
+            rows = xT[a * P * PACK:(a + 1) * P * PACK, :].rearrange("(p j) w -> p j w", j=PACK)
+            nc.sync.dma_start(out=planes[a][t][:], in_=rows[:, t, :])
+
+        nc.gpsimd.memset(gate_rows[:], 0.0)
+        make_identity(nc, ident[:])
+        nc.vector.memset(windows[0][:], 0.0)
+        nc.vector.memset(w_plane[:].bitcast(U32), 0)
+        for m in range(1, ROW_BLOCKS):
+            nc.scalar.activation(windows[m][:], windows[0][:], COPY)
+
+        load_plane(0, 0)
+        nc.sync.dma_start(offsets[:], offs)
+        nc.scalar.dma_start(out=gate_rows[0:E, :], in_=gate[0:1, :].rearrange("o (e c) -> (o e) c", e=E))
+        for a in range(PASSES):
+            for t in range(PACK):
+                if (a, t) != (0, 0):
+                    load_plane(a, t)
+        scale_rows = w_scales.rearrange("e a (q i) n -> i q (e a) n", i=4)
+        for i in range(4):
+            nc.sync.dma_start(
+                out=w_plane[i:P:32, :].bitcast(I32).rearrange("q (j n) -> q j n", j=E * PASSES),
+                in_=scale_rows[i].bitcast(I32),
+            )
+        for e in range(E):
+            nc.sync.dma_start(
+                out=w_codes[e][:].bitcast(I32),
+                in_=w_words[e].rearrange("a p n r -> p a (n r)").bitcast(I32),
+            )
+            if e == 0:
+                nc.sync.dma_start(out=bias[:], in_=b.rearrange("(m p) e -> p m e", p=P))
+
+        gate_ps = psum.tile([P, P], F32, name="gate_ps", tag="back", bufs=2)
+        nc.tensor.transpose(gate_ps[:], gate_rows[:], ident[:])
+        nc.scalar.activation(gate_cols[:], gate_ps[:, 0:E], COPY)
+
+        def gather(a, t, e0, e1, turned):
+            nc.vector.tensor_copy(
+                picked[a][t][:, e0 * C:e1 * C],
+                planes[a][t][:].indirect(offsets[:, e0 * C // 16:e1 * C // 16]),
+            )
+            for e in range(e0, e1):
+                nc.tensor.transpose(turned[e][:, t, :], picked[a][t][:, e * C:(e + 1) * C], ident[:])
+
+        def gate_and_round(a, e, turned_e):
+            gated = keep.tile([P, 2, P, 2], BF16, name="gated%d_%d" % (a, e))
+            nc.scalar.activation(
+                gated[:], turned_e[:].rearrange("s (u r) p -> s u p r", u=2), COPY, scale=gate_cols[:, e:e + 1]
+            )
+            return gated
+
+        def turn_back(gated, e0, e1, grouped, first):
+            back = psum.tile([P, e1 - e0, 2, C], F32, name="back", tag="back", bufs=2)
+            for e in range(e0, e1):
+                words = gated[e][:].rearrange("s u p r -> s (u p r)").bitcast(F32)
+                for u in range(2):
+                    nc.tensor.transpose(back[:, e - e0, u, :], words[:, u * P:(u + 1) * P], ident[:])
+            dst = grouped[:].bitcast(F32).rearrange("p (e s u) -> p e s u", s=C, u=2)
+            nc.scalar.copy(dst[:, e0 - first:e1 - first], back[:].rearrange("p e u s -> p e s u"))
+
+        def quantize(a, e0, e1, grouped):
+            nc.vector.quantize_mx(
+                out=x_codes[a][:, e0 * C:e1 * C].bitcast(FP8X4),
+                scales=x_plane[a][:, e0 * C:e1 * C],
+                in_=grouped[:],
+            )
+
+        def expert_rows(m, e0, e1):
+            acc = psum.tile([P, (e1 - e0) * C], F32, name="acc", tag="acc", bufs=2)
+            act = keep.tile([P, (e1 - e0) * C], F32, name="act%d_%d" % (m, e0))
+            for e in range(e0, e1):
+                cols = slice((e - e0) * C, (e - e0 + 1) * C)
+                for a in range(PASSES):
+                    first = (e * PASSES + a) * N + m * P
+                    nc.tensor.matmul_mx(
+                        out=acc[:, cols],
+                        lhsT=w_codes[e][:, a, m * P * PACK:(m + 1) * P * PACK].bitcast(FP8X4),
+                        lhsT_scale=w_plane[:, first:first + P],
+                        rhs=x_codes[a][:, e * C:(e + 1) * C].bitcast(FP8X4),
+                        rhs_scale=x_plane[a][:, e * C:(e + 1) * C],
+                        start=(a == 0),
+                        stop=(a == PASSES - 1),
+                    )
+            for e in range(e0, e1):
+                cols = slice((e - e0) * C, (e - e0 + 1) * C)
+                nc.scalar.activation(act[:, cols], acc[:, cols], RELU, bias=bias[:, m, e:e + 1])
+            nc.vector.tensor_tensor(
+                windows[m][:].indirect(offsets[:, e0 * C // 16:e1 * C // 16]), act[:], act[:], MULT
+            )
+
+        for a in range(PASSES):
+            last = a == PASSES - 1
+            turned = [psum.tile([P, PACK, P], F32, name="turned", tag="turned", bufs=4) for e in range(E)]
+            for t in range(PACK):
+                if last and t == PACK - 1:
+                    gather(a, t, 0, 1, turned)
+                    gather(a, t, 1, E, turned)
+                else:
+                    gather(a, t, 0, E, turned)
+            if not last:
+                grouped = keep.tile([P, S * PACK], BF16, name="grouped%d" % a, align_bytes=64)
+                gated = []
+                for e0 in range(0, E, 2):
+                    gated.extend([gate_and_round(a, e, turned[e]) for e in (e0, e0 + 1)])
+                    turn_back(gated, e0, e0 + 2, grouped, 0)
+                quantize(a, 0, E, grouped)
+            else:
+                gated = []
+                for e0, e1 in UNITS:
+                    grouped = keep.tile([P, (e1 - e0) * C * PACK], BF16, name="grouped%d_%d" % (a, e0), align_bytes=64)
+                    gated.extend([gate_and_round(a, e, turned[e]) for e in range(e0, e1)])
+                    turn_back(gated, e0, e1, grouped, e0)
+                    quantize(a, e0, e1, grouped)
+                    for m in range(ROW_BLOCKS):
+                        expert_rows(m, e0, e1)
+                        if e1 == E:
+                            nc.sync.dma_start(out=out[m * P:(m + 1) * P, :], in_=windows[m][:])

@@ -24,11 +24,10 @@ MULT = mybir.AluOpType.mult
 FLOPS = 2 * K * N * S
 BYTES = 4 * K * T + E * K * N + E * K * N // 32 + 4 * N * E + 4 * S + 2 * P * S // 16 + 4 * N * T
 
-UNITS = [(0, 1), (1, 2), (2, 4)]
-
 
 def tile_moe_pre_lin_relu2_kernel(tc, xT, w_words, w_scales, b, gate, offs, out):
     nc = tc.nc
+    last = PASSES - 1
     with ExitStack() as ctx:
         keep = ctx.enter_context(tc.tile_pool(name="keep", bufs=1))
         psum = ctx.enter_context(tc.psum_pool(name="psum", bufs=1))
@@ -37,18 +36,36 @@ def tile_moe_pre_lin_relu2_kernel(tc, xT, w_words, w_scales, b, gate, offs, out)
         ident = keep.tile([P, P], F32, name="ident")
         gate_rows = keep.tile([P, P], F32, name="gate_rows")
         gate_cols = keep.tile([P, E], F32, name="gate_cols")
+        gate_first = keep.tile([P, C], F32, name="gate_first")
         bias = keep.tile([P, ROW_BLOCKS, E], F32, name="bias")
         w_plane = keep.tile([P, E * PASSES * N], U8, name="w_plane", align_bytes=64)
         w_codes = [keep.tile([P, PASSES, N * PACK], U8, name="w_codes%d" % e, align_bytes=64) for e in range(E)]
-        planes = [[keep.tile([P, T], F32, name="x%d_%d" % (a, t)) for t in range(PACK)] for a in range(PASSES)]
-        picked = [[keep.tile([P, S], F32, name="g%d_%d" % (a, t)) for t in range(PACK)] for a in range(PASSES)]
         windows = [keep.tile([P, T], F32, name="win%d" % m) for m in range(ROW_BLOCKS)]
-        x_codes = [keep.tile([P, S], U32, name="xc%d" % a, align_bytes=64) for a in range(PASSES)]
         x_plane = [keep.tile([P, S], U8, name="xs%d" % a, align_bytes=64) for a in range(PASSES)]
+        x_codes = {}
+        planes = {}
 
-        def load_plane(a, t):
-            rows = xT[a * P * PACK:(a + 1) * P * PACK, :].rearrange("(p j) w -> p j w", j=PACK)
-            nc.sync.dma_start(out=planes[a][t][:], in_=rows[:, t, :])
+        def load_planes(a, t0, t1):
+            tile = keep.tile([P, (t1 - t0) * T], F32, name="x%d_%d" % (a, t0), tag="x%d_%d" % (a, t0), align_bytes=64)
+            rows = xT[a * P * PACK:(a + 1) * P * PACK, :].rearrange("(p j) w -> p (j w)", j=PACK)
+            nc.sync.dma_start(out=tile[:], in_=rows[:, t0 * T:t1 * T])
+            for t in range(t0, t1):
+                planes[a, t] = tile[:, (t - t0) * T:(t - t0 + 1) * T]
+
+        def load_scales(e0, e1):
+            scale_rows = w_scales[e0:e1].rearrange("e a (q i) n -> i q (e a) n", i=4)
+            cols = slice(e0 * PASSES * N, e1 * PASSES * N)
+            for i in range(4):
+                nc.sync.dma_start(
+                    out=w_plane[i:P:32, cols].bitcast(I32).rearrange("q (j n) -> q j n", j=(e1 - e0) * PASSES),
+                    in_=scale_rows[i].bitcast(I32),
+                )
+
+        def load_codes(e):
+            nc.sync.dma_start(
+                out=w_codes[e][:].bitcast(I32),
+                in_=w_words[e].rearrange("a p n r -> p a (n r)").bitcast(I32),
+            )
 
         nc.gpsimd.memset(gate_rows[:], 0.0)
         make_identity(nc, ident[:])
@@ -57,60 +74,64 @@ def tile_moe_pre_lin_relu2_kernel(tc, xT, w_words, w_scales, b, gate, offs, out)
         for m in range(1, ROW_BLOCKS):
             nc.scalar.activation(windows[m][:], windows[0][:], COPY)
 
-        load_plane(0, 0)
+        load_planes(0, 0, 1)
         nc.sync.dma_start(offsets[:], offs)
         nc.scalar.dma_start(out=gate_rows[0:E, :], in_=gate[0:1, :].rearrange("o (e c) -> (o e) c", e=E))
-        for a in range(PASSES):
-            for t in range(PACK):
-                if (a, t) != (0, 0):
-                    load_plane(a, t)
-        scale_rows = w_scales.rearrange("e a (q i) n -> i q (e a) n", i=4)
-        for i in range(4):
-            nc.sync.dma_start(
-                out=w_plane[i:P:32, :].bitcast(I32).rearrange("q (j n) -> q j n", j=E * PASSES),
-                in_=scale_rows[i].bitcast(I32),
-            )
-        for e in range(E):
-            nc.sync.dma_start(
-                out=w_codes[e][:].bitcast(I32),
-                in_=w_words[e].rearrange("a p n r -> p a (n r)").bitcast(I32),
-            )
-            if e == 0:
-                nc.sync.dma_start(out=bias[:], in_=b.rearrange("(m p) e -> p m e", p=P))
+        for t in range(1, PACK):
+            load_planes(0, t, t + 1)
+        load_planes(1, 0, 1)
+        load_planes(1, 1, 2)
+        nc.sync.dma_start(out=gate_first[:], in_=gate[0:P, 0:C])
+        load_planes(1, 2, 3)
+        load_planes(1, 3, 4)
+        for t in range(PACK):
+            load_planes(last, t, t + 1)
+        load_scales(0, 1)
+        load_codes(0)
+        nc.sync.dma_start(out=bias[:], in_=b.rearrange("(m p) e -> p m e", p=P))
+        load_scales(1, E)
+        for e in range(1, E):
+            load_codes(e)
 
         gate_ps = psum.tile([P, P], F32, name="gate_ps", tag="back", bufs=2)
         nc.tensor.transpose(gate_ps[:], gate_rows[:], ident[:])
         nc.scalar.activation(gate_cols[:], gate_ps[:, 0:E], COPY)
 
-        def gather(a, t, e0, e1, turned):
-            nc.vector.tensor_copy(
-                picked[a][t][:, e0 * C:e1 * C],
-                planes[a][t][:].indirect(offsets[:, e0 * C // 16:e1 * C // 16]),
-            )
-            for e in range(e0, e1):
-                nc.tensor.transpose(turned[e][:, t, :], picked[a][t][:, e * C:(e + 1) * C], ident[:])
+        def entries(e0, e1):
+            return offsets[:, e0 * C // 16:e1 * C // 16]
 
-        def gate_and_round(a, e, turned_e):
-            gated = keep.tile([P, 2, P, 2], BF16, name="gated%d_%d" % (a, e))
-            nc.scalar.activation(
-                gated[:], turned_e[:].rearrange("s (u r) p -> s u p r", u=2), COPY, scale=gate_cols[:, e:e + 1]
-            )
-            return gated
+        def gather(a, t, e0, e1, tag=None):
+            name = "picked%d_%d_%d" % (a, t, e0)
+            picked = keep.tile([P, (e1 - e0) * C], F32, name=name, tag=tag or name, align_bytes=64)
+            nc.vector.tensor_copy(picked[:], planes[a, t].indirect(entries(e0, e1)))
+            return {e: picked[:, (e - e0) * C:(e - e0 + 1) * C] for e in range(e0, e1)}
 
-        def turn_back(gated, e0, e1, grouped, first):
-            back = psum.tile([P, e1 - e0, 2, C], F32, name="back", tag="back", bufs=2)
+        def gate_pair(a, u, pair, e0, e1, back):
+            turned = psum.tile([P, e1 - e0, 2, P], F32, name="turned", tag="turned", bufs=4)
+            for r in range(2):
+                for e in range(e0, e1):
+                    nc.tensor.transpose(turned[:, e - e0, r, :], pair[r][e], ident[:])
+            gated = []
             for e in range(e0, e1):
-                words = gated[e][:].rearrange("s u p r -> s (u p r)").bitcast(F32)
-                for u in range(2):
-                    nc.tensor.transpose(back[:, e - e0, u, :], words[:, u * P:(u + 1) * P], ident[:])
-            dst = grouped[:].bitcast(F32).rearrange("p (e s u) -> p e s u", s=C, u=2)
-            nc.scalar.copy(dst[:, e0 - first:e1 - first], back[:].rearrange("p e u s -> p e s u"))
+                one = keep.tile([P, P, 2], BF16, name="gated%d_%d_%d" % (a, e, u))
+                nc.scalar.activation(
+                    one[:], turned[:, e - e0].rearrange("s r p -> s p r"), COPY, scale=gate_cols[:, e:e + 1]
+                )
+                gated.append(one)
+            for e in range(e0, e1):
+                words = gated[e - e0][:].rearrange("s p r -> s (p r)").bitcast(F32)
+                nc.tensor.transpose(back[:, e - e0, u, :], words, ident[:])
+
+        def weave(back, dst):
+            nc.scalar.copy(
+                dst.bitcast(F32).rearrange("p (e s u) -> p e s u", s=C, u=2), back[:].rearrange("p e u s -> p e s u")
+            )
 
         def quantize(a, e0, e1, grouped):
             nc.vector.quantize_mx(
                 out=x_codes[a][:, e0 * C:e1 * C].bitcast(FP8X4),
                 scales=x_plane[a][:, e0 * C:e1 * C],
-                in_=grouped[:],
+                in_=grouped,
             )
 
         def expert_rows(m, e0, e1):
@@ -127,39 +148,62 @@ def tile_moe_pre_lin_relu2_kernel(tc, xT, w_words, w_scales, b, gate, offs, out)
                         rhs=x_codes[a][:, e * C:(e + 1) * C].bitcast(FP8X4),
                         rhs_scale=x_plane[a][:, e * C:(e + 1) * C],
                         start=(a == 0),
-                        stop=(a == PASSES - 1),
+                        stop=(a == last),
                     )
             for e in range(e0, e1):
                 cols = slice((e - e0) * C, (e - e0 + 1) * C)
                 nc.scalar.activation(act[:, cols], acc[:, cols], RELU, bias=bias[:, m, e:e + 1])
-            nc.vector.tensor_tensor(
-                windows[m][:].indirect(offsets[:, e0 * C // 16:e1 * C // 16]), act[:], act[:], MULT
-            )
+            nc.vector.tensor_tensor(windows[m][:].indirect(entries(e0, e1)), act[:], act[:], MULT)
 
-        for a in range(PASSES):
-            last = a == PASSES - 1
-            turned = [psum.tile([P, PACK, P], F32, name="turned", tag="turned", bufs=4) for e in range(E)]
-            for t in range(PACK):
-                if last and t == PACK - 1:
-                    gather(a, t, 0, 1, turned)
-                    gather(a, t, 1, E, turned)
-                else:
-                    gather(a, t, 0, E, turned)
-            if not last:
-                grouped = keep.tile([P, S * PACK], BF16, name="grouped%d" % a, align_bytes=64)
-                gated = []
-                for e0 in range(0, E, 2):
-                    gated.extend([gate_and_round(a, e, turned[e]) for e in (e0, e0 + 1)])
-                    turn_back(gated, e0, e0 + 2, grouped, 0)
-                quantize(a, 0, E, grouped)
-            else:
-                gated = []
-                for e0, e1 in UNITS:
-                    grouped = keep.tile([P, (e1 - e0) * C * PACK], BF16, name="grouped%d_%d" % (a, e0), align_bytes=64)
-                    gated.extend([gate_and_round(a, e, turned[e]) for e in range(e0, e1)])
-                    turn_back(gated, e0, e1, grouped, e0)
-                    quantize(a, e0, e1, grouped)
-                    for m in range(ROW_BLOCKS):
-                        expert_rows(m, e0, e1)
-                        if e1 == E:
-                            nc.sync.dma_start(out=out[m * P:(m + 1) * P, :], in_=windows[m][:])
+        grouped = {}
+        for a in range(last):
+            grouped[a] = keep.tile([P, S * PACK], BF16, name="grouped%d" % a, align_bytes=64)
+            backs = [psum.tile([P, 2, 2, C], F32, name="back", tag="back", bufs=2) for h in range(2)]
+            for u in range(2):
+                pair = [gather(a, 2 * u + r, 0, E) for r in range(2)]
+                for h in range(2):
+                    gate_pair(a, u, pair, 2 * h, 2 * h + 2, backs[h])
+            for h in range(2):
+                weave(backs[h], grouped[a][:, h * 2 * C * PACK:(h + 1) * 2 * C * PACK])
+
+        x_codes[0] = keep.tile([P, S], U32, name="xc0", tag="x1_3", align_bytes=64)
+        quantize(0, 0, E, grouped[0][:])
+
+        direct = keep.tile([P, PACK, C], F32, name="direct")
+        units = [(1, 2), (2, E)]
+        backs = [psum.tile([P, e1 - e0, 2, C], F32, name="back", tag="back", bufs=2) for e0, e1 in units]
+
+        def gather_gated(t):
+            nc.vector.tensor_tensor(direct[:, t, :], planes[last, t].indirect(entries(0, 1)), gate_first[:], MULT)
+
+        pair = []
+        for t in range(2):
+            gather_gated(t)
+            pair.append(gather(last, t, 1, E))
+        for back, (e0, e1) in zip(backs, units):
+            gate_pair(last, 0, pair, e0, e1, back)
+        gather_gated(2)
+        third = gather(last, 2, 1, E)
+        x_codes[1] = keep.tile([P, S], U32, name="xc1", tag="x%d_2" % last, align_bytes=64)
+        quantize(1, 0, E, grouped[1][:])
+
+        x_codes[last] = keep.tile([P, S], U32, name="xc2", align_bytes=64)
+        gather_gated(3)
+        grouped_first = keep.tile([P, C * PACK], BF16, name="grouped_first", tag="first", align_bytes=64)
+        nc.vector.tensor_copy(
+            grouped_first[:].rearrange("p (c i t) -> p c t i", i=4, t=PACK),
+            direct[:].rearrange("p t (c i) -> p c t i", i=4),
+        )
+        gate_pair(last, 1, [third, gather(last, 3, 1, 2)], 1, 2, backs[0])
+        quantize(last, 0, 1, grouped_first[:])
+        gate_pair(last, 1, [third, gather(last, 3, 2, E, tag="first")], 2, E, backs[1])
+        for m in range(ROW_BLOCKS):
+            expert_rows(m, 0, 1)
+        for back, (e0, e1) in zip(backs, units):
+            grouped_unit = keep.tile([P, (e1 - e0) * C * PACK], BF16, name="grouped_unit%d" % e0, align_bytes=64)
+            weave(back, grouped_unit[:])
+            quantize(last, e0, e1, grouped_unit[:])
+            for m in range(ROW_BLOCKS):
+                expert_rows(m, e0, e1)
+                if e1 == E:
+                    nc.sync.dma_start(out=out[m * P:(m + 1) * P, :], in_=windows[m][:])

@@ -8,7 +8,11 @@ S = E * C
 P = 128
 PACK = 4
 PASSES = K // (P * PACK)
+LAST = PASSES - 1
 ROW_BLOCKS = N // P
+GROUP = 16
+QUADRANT = 32
+LIVE_ROWS = 4
 
 F32 = mybir.dt.float32
 BF16 = mybir.dt.bfloat16
@@ -22,42 +26,41 @@ RELU = mybir.ActivationFunctionType.Relu
 MULT = mybir.AluOpType.mult
 
 FLOPS = 2 * K * N * S
-BYTES = 4 * K * T + E * K * N + E * K * N // 32 + 4 * N * E + 4 * S + 2 * P * S // 16 + 4 * N * T
+BYTES = 4 * K * T + E * K * N + E * K * N // 32 + 4 * N * E + 4 * S + 2 * P * S // GROUP + 4 * N * T
 
 
 def tile_moe_pre_lin_relu2_kernel(tc, xT, w_words, w_scales, b, gate, offs, out):
     nc = tc.nc
-    last = PASSES - 1
     with ExitStack() as ctx:
         keep = ctx.enter_context(tc.tile_pool(name="keep", bufs=1))
         psum = ctx.enter_context(tc.psum_pool(name="psum", bufs=1))
 
-        offsets = keep.tile([P, S // 16], U16, name="offsets")
+        offsets = keep.tile([P, S // GROUP], U16, name="offsets")
         ident = keep.tile([P, P], F32, name="ident")
         gate_rows = keep.tile([P, P], F32, name="gate_rows")
         gate_cols = keep.tile([P, E], F32, name="gate_cols")
-        gate_first = keep.tile([P, C], F32, name="gate_first")
         bias = keep.tile([P, ROW_BLOCKS, E], F32, name="bias")
-        w_plane = keep.tile([P, E * PASSES * N], U8, name="w_plane", align_bytes=64)
+        w_scale_bytes = keep.tile([P, E * PASSES * N], U8, name="w_scale_bytes", align_bytes=64)
         w_codes = [keep.tile([P, PASSES, N * PACK], U8, name="w_codes%d" % e, align_bytes=64) for e in range(E)]
-        windows = [keep.tile([P, T], F32, name="win%d" % m) for m in range(ROW_BLOCKS)]
-        x_plane = [keep.tile([P, S], U8, name="xs%d" % a, align_bytes=64) for a in range(PASSES)]
+        windows = [keep.tile([P, T], F32, name="window%d" % m) for m in range(ROW_BLOCKS)]
+        x_scale_bytes = [keep.tile([P, S], U8, name="x_scale_bytes%d" % a, align_bytes=64) for a in range(PASSES)]
         x_codes = {}
         planes = {}
 
-        def load_planes(a, t0, t1):
-            tile = keep.tile([P, (t1 - t0) * T], F32, name="x%d_%d" % (a, t0), tag="x%d_%d" % (a, t0), align_bytes=64)
-            rows = xT[a * P * PACK:(a + 1) * P * PACK, :].rearrange("(p j) w -> p (j w)", j=PACK)
-            nc.sync.dma_start(out=tile[:], in_=rows[:, t0 * T:t1 * T])
-            for t in range(t0, t1):
-                planes[a, t] = tile[:, (t - t0) * T:(t - t0 + 1) * T]
+        def load_plane(a, t):
+            name = "plane%d_%d" % (a, t)
+            plane = keep.tile([P, T], F32, name=name, tag=name, align_bytes=64)
+            rows = xT[a * P * PACK:(a + 1) * P * PACK, :].rearrange("(p j) w -> p j w", j=PACK)
+            nc.sync.dma_start(out=plane[:], in_=rows[:, t, :])
+            planes[a, t] = plane[:]
 
         def load_scales(e0, e1):
-            scale_rows = w_scales[e0:e1].rearrange("e a (q i) n -> i q (e a) n", i=4)
+            scale_rows = w_scales[e0:e1].rearrange("e a (q i) n -> i q (e a) n", i=LIVE_ROWS)
             cols = slice(e0 * PASSES * N, e1 * PASSES * N)
-            for i in range(4):
+            for i in range(LIVE_ROWS):
+                dst = w_scale_bytes[i:P:QUADRANT, cols].bitcast(I32)
                 nc.sync.dma_start(
-                    out=w_plane[i:P:32, cols].bitcast(I32).rearrange("q (j n) -> q j n", j=(e1 - e0) * PASSES),
+                    out=dst.rearrange("q (j n) -> q j n", j=(e1 - e0) * PASSES),
                     in_=scale_rows[i].bitcast(I32),
                 )
 
@@ -70,140 +73,163 @@ def tile_moe_pre_lin_relu2_kernel(tc, xT, w_words, w_scales, b, gate, offs, out)
         nc.gpsimd.memset(gate_rows[:], 0.0)
         make_identity(nc, ident[:])
         nc.vector.memset(windows[0][:], 0.0)
-        nc.vector.memset(w_plane[:].bitcast(U32), 0)
+        nc.vector.memset(w_scale_bytes[:].bitcast(U32), 0)
         for m in range(1, ROW_BLOCKS):
             nc.scalar.activation(windows[m][:], windows[0][:], COPY)
 
-        load_planes(0, 0, 1)
+        load_plane(0, 0)
         nc.sync.dma_start(offsets[:], offs)
         nc.scalar.dma_start(out=gate_rows[0:E, :], in_=gate[0:1, :].rearrange("o (e c) -> (o e) c", e=E))
-        for t in range(1, PACK):
-            load_planes(0, t, t + 1)
-        load_planes(1, 0, 1)
-        load_planes(1, 1, 2)
-        nc.sync.dma_start(out=gate_first[:], in_=gate[0:P, 0:C])
-        load_planes(1, 2, 3)
-        load_planes(1, 3, 4)
-        for t in range(PACK):
-            load_planes(last, t, t + 1)
+        for a in range(PASSES):
+            for t in range(PACK):
+                if (a, t) != (0, 0):
+                    load_plane(a, t)
         load_scales(0, 1)
         load_codes(0)
         nc.sync.dma_start(out=bias[:], in_=b.rearrange("(m p) e -> p m e", p=P))
-        load_scales(1, E)
-        for e in range(1, E):
+        load_scales(1, 2)
+        load_codes(1)
+        load_scales(2, E)
+        for e in range(2, E):
             load_codes(e)
 
-        gate_ps = psum.tile([P, P], F32, name="gate_ps", tag="back", bufs=2)
+        def bank_tile(bank, shape):
+            return psum.tile(shape, F32, name="bank%d" % bank, tag="bank%d" % bank)
+
+        gate_ps = bank_tile(6, [P, P])
         nc.tensor.transpose(gate_ps[:], gate_rows[:], ident[:])
         nc.scalar.activation(gate_cols[:], gate_ps[:, 0:E], COPY)
+        gate_first = keep.tile([P, C], F32, name="gate_first")
+        spread_ps = bank_tile(7, [P, C])
+        nc.tensor.transpose(spread_ps[:], gate_cols[:, 0:1].to_broadcast([P, P]), ident[:])
+        nc.scalar.activation(gate_first[:], spread_ps[:], COPY)
 
         def entries(e0, e1):
-            return offsets[:, e0 * C // 16:e1 * C // 16]
+            return offsets[:, e0 * C // GROUP:e1 * C // GROUP]
 
-        def gather(a, t, e0, e1, tag=None):
-            name = "picked%d_%d_%d" % (a, t, e0)
-            picked = keep.tile([P, (e1 - e0) * C], F32, name=name, tag=tag or name, align_bytes=64)
-            nc.vector.tensor_copy(picked[:], planes[a, t].indirect(entries(e0, e1)))
+        def gather_into(picked, plane, e0, e1):
+            nc.vector.tensor_copy(picked, plane.indirect(entries(e0, e1)))
             return {e: picked[:, (e - e0) * C:(e - e0 + 1) * C] for e in range(e0, e1)}
 
-        def gate_pair(a, u, pair, e0, e1, back):
-            turned = psum.tile([P, e1 - e0, 2, P], F32, name="turned", tag="turned", bufs=4)
+        def gather(a, t, e0, e1):
+            name = "picked%d_%d_%d" % (a, t, e0)
+            picked = keep.tile([P, (e1 - e0) * C], F32, name=name, tag=name, align_bytes=64)
+            return gather_into(picked[:], planes[a, t], e0, e1)
+
+        def gate_pair(a, u, pair, e0, e1, bank):
+            turned = bank_tile(bank, [P, e1 - e0, 2, P])
             for r in range(2):
                 for e in range(e0, e1):
                     nc.tensor.transpose(turned[:, e - e0, r, :], pair[r][e], ident[:])
             gated = []
             for e in range(e0, e1):
-                one = keep.tile([P, P, 2], BF16, name="gated%d_%d_%d" % (a, e, u))
+                name = "gated%d_%d_%d" % (a, e, u)
+                rounded = keep.tile([P, P, 2], BF16, name=name, tag=name)
                 nc.scalar.activation(
-                    one[:], turned[:, e - e0].rearrange("s r p -> s p r"), COPY, scale=gate_cols[:, e:e + 1]
+                    rounded[:], turned[:, e - e0].rearrange("s r p -> s p r"), COPY, scale=gate_cols[:, e:e + 1]
                 )
-                gated.append(one)
-            for e in range(e0, e1):
-                words = gated[e - e0][:].rearrange("s p r -> s (p r)").bitcast(F32)
-                nc.tensor.transpose(back[:, e - e0, u, :], words, ident[:])
+                gated.append(rounded)
+            return gated
+
+        def turn_back(gated, u, back):
+            for i, rounded in enumerate(gated):
+                words = rounded[:].rearrange("s p r -> s (p r)").bitcast(F32)
+                nc.tensor.transpose(back[:, i, u, :], words, ident[:])
 
         def weave(back, dst):
             nc.scalar.copy(
                 dst.bitcast(F32).rearrange("p (e s u) -> p e s u", s=C, u=2), back[:].rearrange("p e u s -> p e s u")
             )
 
-        def quantize(a, e0, e1, grouped):
+        def quantize(a, e0, e1, woven):
             nc.vector.quantize_mx(
                 out=x_codes[a][:, e0 * C:e1 * C].bitcast(FP8X4),
-                scales=x_plane[a][:, e0 * C:e1 * C],
-                in_=grouped,
+                scales=x_scale_bytes[a][:, e0 * C:e1 * C],
+                in_=woven,
             )
 
-        def expert_rows(m, e0, e1):
-            acc = psum.tile([P, (e1 - e0) * C], F32, name="acc", tag="acc", bufs=2)
-            act = keep.tile([P, (e1 - e0) * C], F32, name="act%d_%d" % (m, e0))
+        def expert_rows(m, e0, e1, bank, tag=None):
+            acc = bank_tile(bank, [P, (e1 - e0) * C])
+            name = "act%d_%d" % (m, e0)
+            act = keep.tile([P, (e1 - e0) * C], F32, name=name, tag=tag or name)
             for e in range(e0, e1):
                 cols = slice((e - e0) * C, (e - e0 + 1) * C)
                 for a in range(PASSES):
-                    first = (e * PASSES + a) * N + m * P
+                    scale_col = (e * PASSES + a) * N + m * P
                     nc.tensor.matmul_mx(
                         out=acc[:, cols],
                         lhsT=w_codes[e][:, a, m * P * PACK:(m + 1) * P * PACK].bitcast(FP8X4),
-                        lhsT_scale=w_plane[:, first:first + P],
+                        lhsT_scale=w_scale_bytes[:, scale_col:scale_col + P],
                         rhs=x_codes[a][:, e * C:(e + 1) * C].bitcast(FP8X4),
-                        rhs_scale=x_plane[a][:, e * C:(e + 1) * C],
+                        rhs_scale=x_scale_bytes[a][:, e * C:(e + 1) * C],
                         start=(a == 0),
-                        stop=(a == last),
+                        stop=(a == LAST),
                     )
             for e in range(e0, e1):
                 cols = slice((e - e0) * C, (e - e0 + 1) * C)
                 nc.scalar.activation(act[:, cols], acc[:, cols], RELU, bias=bias[:, m, e:e + 1])
             nc.vector.tensor_tensor(windows[m][:].indirect(entries(e0, e1)), act[:], act[:], MULT)
 
-        grouped = {}
-        for a in range(last):
-            grouped[a] = keep.tile([P, S * PACK], BF16, name="grouped%d" % a, align_bytes=64)
-            backs = [psum.tile([P, 2, 2, C], F32, name="back", tag="back", bufs=2) for h in range(2)]
+        woven = {}
+        for a in range(LAST):
+            woven[a] = keep.tile([P, S * PACK], BF16, name="woven%d" % a, align_bytes=64)
+            backs = [bank_tile(4 + h, [P, 2, 2, C]) for h in range(2)]
             for u in range(2):
                 pair = [gather(a, 2 * u + r, 0, E) for r in range(2)]
                 for h in range(2):
-                    gate_pair(a, u, pair, 2 * h, 2 * h + 2, backs[h])
+                    turn_back(gate_pair(a, u, pair, 2 * h, 2 * h + 2, 2 * u + h), u, backs[h])
             for h in range(2):
-                weave(backs[h], grouped[a][:, h * 2 * C * PACK:(h + 1) * 2 * C * PACK])
+                weave(backs[h], woven[a][:, h * 2 * C * PACK:(h + 1) * 2 * C * PACK])
 
-        x_codes[0] = keep.tile([P, S], U32, name="xc0", tag="x1_3", align_bytes=64)
-        quantize(0, 0, E, grouped[0][:])
+        x_codes[0] = keep.tile([P, S], U32, name="x_codes0", tag="plane1_3", align_bytes=64)
+        quantize(0, 0, E, woven[0][:])
 
-        direct = keep.tile([P, PACK, C], F32, name="direct")
-        units = [(1, 2), (2, E)]
-        backs = [psum.tile([P, e1 - e0, 2, C], F32, name="back", tag="back", bufs=2) for e0, e1 in units]
+        first_gated = keep.tile([P, PACK, C], F32, name="first_gated")
 
-        def gather_gated(t):
-            nc.vector.tensor_tensor(direct[:, t, :], planes[last, t].indirect(entries(0, 1)), gate_first[:], MULT)
+        def gather_first(t):
+            nc.vector.tensor_tensor(first_gated[:, t, :], planes[LAST, t].indirect(entries(0, 1)), gate_first[:], MULT)
 
-        pair = []
+        low = []
         for t in range(2):
-            gather_gated(t)
-            pair.append(gather(last, t, 1, E))
-        for back, (e0, e1) in zip(backs, units):
-            gate_pair(last, 0, pair, e0, e1, back)
-        gather_gated(2)
-        third = gather(last, 2, 1, E)
-        x_codes[1] = keep.tile([P, S], U32, name="xc1", tag="x%d_2" % last, align_bytes=64)
-        quantize(1, 0, E, grouped[1][:])
-
-        x_codes[last] = keep.tile([P, S], U32, name="xc2", align_bytes=64)
-        gather_gated(3)
-        grouped_first = keep.tile([P, C * PACK], BF16, name="grouped_first", tag="first", align_bytes=64)
+            low.append(gather(LAST, t, 1, E))
+            gather_first(t)
+        back_second = bank_tile(4, [P, 1, 2, C])
+        turn_back(gate_pair(LAST, 0, low, 1, 2, 0), 0, back_second)
+        rest_low = gate_pair(LAST, 0, low, 2, E, 1)
+        second_high = gather(LAST, 2, 1, 2)
+        gather_first(2)
+        gather_first(3)
+        woven_first = keep.tile([P, C * PACK], BF16, name="woven_first", tag="first", align_bytes=64)
         nc.vector.tensor_copy(
-            grouped_first[:].rearrange("p (c i t) -> p c t i", i=4, t=PACK),
-            direct[:].rearrange("p t (c i) -> p c t i", i=4),
+            woven_first[:].rearrange("p (c i t) -> p c t i", i=4, t=PACK),
+            first_gated[:].rearrange("p t (c i) -> p c t i", i=4),
         )
-        gate_pair(last, 1, [third, gather(last, 3, 1, 2)], 1, 2, backs[0])
-        quantize(last, 0, 1, grouped_first[:])
-        gate_pair(last, 1, [third, gather(last, 3, 2, E, tag="first")], 2, E, backs[1])
+        turn_back(gate_pair(LAST, 1, [second_high, gather(LAST, 3, 1, 2)], 1, 2, 2), 1, back_second)
+        x_codes[1] = keep.tile([P, S], U32, name="x_codes1", tag="picked%d_2_1" % LAST, align_bytes=64)
+        quantize(1, 0, E, woven[1][:])
+        x_codes[LAST] = keep.tile([P, S], U32, name="x_codes2", align_bytes=64)
+        quantize(LAST, 0, 1, woven_first[:])
+
+        rest_picked = keep.tile([P, 2, 2 * C], F32, name="rest_picked", tag="first", align_bytes=64)
+        rest_pair = [gather_into(rest_picked[:, r, :], planes[LAST, 2 + r], 2, E) for r in range(2)]
+        woven_second = keep.tile([P, C * PACK], BF16, name="woven_second", align_bytes=64)
+        weave(back_second, woven_second[:])
+        quantize(LAST, 1, 2, woven_second[:])
+
+        expert_rows(0, 0, 1, 6)
+        expert_rows(1, 0, 1, 5)
+        rest_high = gate_pair(LAST, 1, rest_pair, 2, E, 6)
+        expert_rows(0, 1, 2, 7)
+        back_rest = bank_tile(7, [P, 2, 2, C])
+        turn_back(rest_low, 0, back_rest)
+        turn_back(rest_high, 1, back_rest)
+        expert_rows(1, 1, 2, 0)
+        woven_rest = keep.tile([P, 2 * C * PACK], BF16, name="woven_rest", align_bytes=64)
+        weave(back_rest, woven_rest[:])
+        quantize(LAST, 2, E, woven_rest[:])
+        expert_rows(2, 0, 2, 1, tag="gated%d_3_1" % LAST)
+        expert_rows(0, 2, 3, 2)
+        expert_rows(1, 2, 3, 3)
         for m in range(ROW_BLOCKS):
-            expert_rows(m, 0, 1)
-        for back, (e0, e1) in zip(backs, units):
-            grouped_unit = keep.tile([P, (e1 - e0) * C * PACK], BF16, name="grouped_unit%d" % e0, align_bytes=64)
-            weave(back, grouped_unit[:])
-            quantize(last, e0, e1, grouped_unit[:])
-            for m in range(ROW_BLOCKS):
-                expert_rows(m, e0, e1)
-                if e1 == E:
-                    nc.sync.dma_start(out=out[m * P:(m + 1) * P, :], in_=windows[m][:])
+            expert_rows(m, 3 if m < 2 else 2, E, 4 + m)
+            nc.sync.dma_start(out=out[m * P:(m + 1) * P, :], in_=windows[m][:])

from contextlib import ExitStack

import concourse.mybir as mybir
from concourse.masks import make_identity

K, T, E, C, N = 1536, 1024, 4, 128, 384
S = E * C
P = 128
PACK = 4
PASSES = K // (P * PACK)
LAST = PASSES - 1
ROW_BLOCKS = N // P
GROUP = 16
QUADRANT = 32
LIVE_ROWS = 4

F32 = mybir.dt.float32
BF16 = mybir.dt.bfloat16
I32 = mybir.dt.int32
U32 = mybir.dt.uint32
U16 = mybir.dt.uint16
U8 = mybir.dt.uint8
FP8X4 = mybir.dt.float8_e4m3fn_x4
COPY = mybir.ActivationFunctionType.Copy
RELU = mybir.ActivationFunctionType.Relu
MULT = mybir.AluOpType.mult

FLOPS = 2 * K * N * S
BYTES = 4 * K * T + E * K * N + E * K * N // 32 + 4 * N * E + 4 * S + 2 * P * S // GROUP + 4 * N * T


def tile_moe_pre_lin_relu2_kernel(tc, xT, w_words, w_scales, b, gate, offs, out):
    nc = tc.nc
    with ExitStack() as ctx:
        keep = ctx.enter_context(tc.tile_pool(name="keep", bufs=1))
        psum = ctx.enter_context(tc.psum_pool(name="psum", bufs=1))

        offsets = keep.tile([P, S // GROUP], U16, name="offsets")
        ident = keep.tile([P, P], F32, name="ident")
        gate_rows = keep.tile([P, P], F32, name="gate_rows")
        gate_cols = keep.tile([P, E], F32, name="gate_cols")
        bias = keep.tile([P, ROW_BLOCKS, E], F32, name="bias")
        w_scale_bytes = keep.tile([P, E * PASSES * N], U8, name="w_scale_bytes", align_bytes=64)
        w_codes = [keep.tile([P, PASSES, N * PACK], U8, name="w_codes%d" % e, align_bytes=64) for e in range(E)]
        windows = [keep.tile([P, T], F32, name="window%d" % m) for m in range(ROW_BLOCKS)]
        x_scale_bytes = [keep.tile([P, S], U8, name="x_scale_bytes%d" % a, align_bytes=64) for a in range(PASSES)]
        x_codes = {}
        planes = {}

        def load_plane(a, t):
            name = "plane%d_%d" % (a, t)
            plane = keep.tile([P, T], F32, name=name, tag=name, align_bytes=64)
            rows = xT[a * P * PACK:(a + 1) * P * PACK, :].rearrange("(p j) w -> p j w", j=PACK)
            nc.sync.dma_start(out=plane[:], in_=rows[:, t, :])
            planes[a, t] = plane[:]

        def load_scales(e0, e1):
            scale_rows = w_scales[e0:e1].rearrange("e a (q i) n -> i q (e a) n", i=LIVE_ROWS)
            cols = slice(e0 * PASSES * N, e1 * PASSES * N)
            for i in range(LIVE_ROWS):
                dst = w_scale_bytes[i:P:QUADRANT, cols].bitcast(I32)
                nc.sync.dma_start(
                    out=dst.rearrange("q (j n) -> q j n", j=(e1 - e0) * PASSES),
                    in_=scale_rows[i].bitcast(I32),
                )

        def load_codes(e):
            nc.sync.dma_start(
                out=w_codes[e][:].bitcast(I32),
                in_=w_words[e].rearrange("a p n r -> p a (n r)").bitcast(I32),
            )

        nc.gpsimd.memset(gate_rows[:], 0.0)
        make_identity(nc, ident[:])
        nc.vector.memset(windows[0][:], 0.0)
        nc.vector.memset(w_scale_bytes[:].bitcast(U32), 0)
        for m in range(1, ROW_BLOCKS):
            nc.scalar.activation(windows[m][:], windows[0][:], COPY)

        load_plane(0, 0)
        nc.sync.dma_start(offsets[:], offs)
        nc.scalar.dma_start(out=gate_rows[0:E, :], in_=gate[0:1, :].rearrange("o (e c) -> (o e) c", e=E))
        for a in range(PASSES):
            for t in range(PACK):
                if (a, t) != (0, 0):
                    load_plane(a, t)
        load_scales(0, 1)
        load_codes(0)
        nc.sync.dma_start(out=bias[:], in_=b.rearrange("(m p) e -> p m e", p=P))
        load_scales(1, 2)
        load_codes(1)
        load_scales(2, E)
        for e in range(2, E):
            load_codes(e)

        def bank_tile(bank, shape):
            return psum.tile(shape, F32, name="bank%d" % bank, tag="bank%d" % bank)

        gate_ps = bank_tile(6, [P, P])
        nc.tensor.transpose(gate_ps[:], gate_rows[:], ident[:])
        nc.scalar.activation(gate_cols[:], gate_ps[:, 0:E], COPY)
        gate_first = keep.tile([P, C], F32, name="gate_first")
        spread_ps = bank_tile(7, [P, C])
        nc.tensor.transpose(spread_ps[:], gate_cols[:, 0:1].to_broadcast([P, P]), ident[:])
        nc.scalar.activation(gate_first[:], spread_ps[:], COPY)

        def entries(e0, e1):
            return offsets[:, e0 * C // GROUP:e1 * C // GROUP]

        def gather_into(picked, plane, e0, e1):
            nc.vector.tensor_copy(picked, plane.indirect(entries(e0, e1)))
            return {e: picked[:, (e - e0) * C:(e - e0 + 1) * C] for e in range(e0, e1)}

        def gather(a, t, e0, e1):
            name = "picked%d_%d_%d" % (a, t, e0)
            picked = keep.tile([P, (e1 - e0) * C], F32, name=name, tag=name, align_bytes=64)
            return gather_into(picked[:], planes[a, t], e0, e1)

        def gate_pair(a, u, pair, e0, e1, bank):
            turned = bank_tile(bank, [P, e1 - e0, 2, P])
            for r in range(2):
                for e in range(e0, e1):
                    nc.tensor.transpose(turned[:, e - e0, r, :], pair[r][e], ident[:])
            gated = []
            for e in range(e0, e1):
                name = "gated%d_%d_%d" % (a, e, u)
                rounded = keep.tile([P, P, 2], BF16, name=name, tag=name)
                nc.scalar.activation(
                    rounded[:], turned[:, e - e0].rearrange("s r p -> s p r"), COPY, scale=gate_cols[:, e:e + 1]
                )
                gated.append(rounded)
            return gated

        def turn_back(gated, u, back):
            for i, rounded in enumerate(gated):
                words = rounded[:].rearrange("s p r -> s (p r)").bitcast(F32)
                nc.tensor.transpose(back[:, i, u, :], words, ident[:])

        def weave(back, dst):
            nc.scalar.copy(
                dst.bitcast(F32).rearrange("p (e s u) -> p e s u", s=C, u=2), back[:].rearrange("p e u s -> p e s u")
            )

        def quantize(a, e0, e1, woven):
            nc.vector.quantize_mx(
                out=x_codes[a][:, e0 * C:e1 * C].bitcast(FP8X4),
                scales=x_scale_bytes[a][:, e0 * C:e1 * C],
                in_=woven,
            )

        def expert_rows(m, e0, e1, bank, tag=None):
            acc = bank_tile(bank, [P, (e1 - e0) * C])
            name = "act%d_%d" % (m, e0)
            act = keep.tile([P, (e1 - e0) * C], F32, name=name, tag=tag or name)
            for e in range(e0, e1):
                cols = slice((e - e0) * C, (e - e0 + 1) * C)
                for a in range(PASSES):
                    scale_col = (e * PASSES + a) * N + m * P
                    nc.tensor.matmul_mx(
                        out=acc[:, cols],
                        lhsT=w_codes[e][:, a, m * P * PACK:(m + 1) * P * PACK].bitcast(FP8X4),
                        lhsT_scale=w_scale_bytes[:, scale_col:scale_col + P],
                        rhs=x_codes[a][:, e * C:(e + 1) * C].bitcast(FP8X4),
                        rhs_scale=x_scale_bytes[a][:, e * C:(e + 1) * C],
                        start=(a == 0),
                        stop=(a == LAST),
                    )
            for e in range(e0, e1):
                cols = slice((e - e0) * C, (e - e0 + 1) * C)
                nc.scalar.activation(act[:, cols], acc[:, cols], RELU, bias=bias[:, m, e:e + 1])
            nc.vector.tensor_tensor(windows[m][:].indirect(entries(e0, e1)), act[:], act[:], MULT)

        woven = {}
        for a in range(LAST):
            woven[a] = keep.tile([P, S * PACK], BF16, name="woven%d" % a, align_bytes=64)
            backs = [bank_tile(4 + h, [P, 2, 2, C]) for h in range(2)]
            for u in range(2):
                pair = [gather(a, 2 * u + r, 0, E) for r in range(2)]
                for h in range(2):
                    turn_back(gate_pair(a, u, pair, 2 * h, 2 * h + 2, 2 * u + h), u, backs[h])
            for h in range(2):
                weave(backs[h], woven[a][:, h * 2 * C * PACK:(h + 1) * 2 * C * PACK])

        x_codes[0] = keep.tile([P, S], U32, name="x_codes0", tag="plane1_3", align_bytes=64)
        quantize(0, 0, E, woven[0][:])

        first_gated = keep.tile([P, PACK, C], F32, name="first_gated")

        def gather_first(t):
            nc.vector.tensor_tensor(first_gated[:, t, :], planes[LAST, t].indirect(entries(0, 1)), gate_first[:], MULT)

        low = []
        for t in range(2):
            low.append(gather(LAST, t, 1, E))
            gather_first(t)
        back_second = bank_tile(4, [P, 1, 2, C])
        turn_back(gate_pair(LAST, 0, low, 1, 2, 0), 0, back_second)
        rest_low = gate_pair(LAST, 0, low, 2, E, 1)
        second_high = gather(LAST, 2, 1, 2)
        gather_first(2)
        gather_first(3)
        woven_first = keep.tile([P, C * PACK], BF16, name="woven_first", tag="first", align_bytes=64)
        nc.vector.tensor_copy(
            woven_first[:].rearrange("p (c i t) -> p c t i", i=4, t=PACK),
            first_gated[:].rearrange("p t (c i) -> p c t i", i=4),
        )
        turn_back(gate_pair(LAST, 1, [second_high, gather(LAST, 3, 1, 2)], 1, 2, 2), 1, back_second)
        x_codes[1] = keep.tile([P, S], U32, name="x_codes1", tag="picked%d_2_1" % LAST, align_bytes=64)
        quantize(1, 0, E, woven[1][:])
        x_codes[LAST] = keep.tile([P, S], U32, name="x_codes2", align_bytes=64)
        quantize(LAST, 0, 1, woven_first[:])

        rest_picked = keep.tile([P, 2, 2 * C], F32, name="rest_picked", tag="first", align_bytes=64)
        rest_pair = [gather_into(rest_picked[:, r, :], planes[LAST, 2 + r], 2, E) for r in range(2)]
        woven_second = keep.tile([P, C * PACK], BF16, name="woven_second", align_bytes=64)
        weave(back_second, woven_second[:])
        quantize(LAST, 1, 2, woven_second[:])

        expert_rows(0, 0, 1, 6)
        expert_rows(1, 0, 1, 5)
        rest_high = gate_pair(LAST, 1, rest_pair, 2, E, 6)
        expert_rows(0, 1, 2, 7)
        back_rest = bank_tile(7, [P, 2, 2, C])
        turn_back(rest_low, 0, back_rest)
        turn_back(rest_high, 1, back_rest)
        expert_rows(1, 1, 2, 0)
        woven_rest = keep.tile([P, 2 * C * PACK], BF16, name="woven_rest", align_bytes=64)
        weave(back_rest, woven_rest[:])
        quantize(LAST, 2, E, woven_rest[:])
        expert_rows(2, 0, 2, 1, tag="gated%d_3_1" % LAST)
        expert_rows(0, 2, 3, 2)
        expert_rows(1, 2, 3, 3)
        for m in range(ROW_BLOCKS):
            expert_rows(m, 3 if m < 2 else 2, E, 4 + m)
            nc.sync.dma_start(out=out[m * P:(m + 1) * P, :], in_=windows[m][:])
